import numpy as np
import ml_dtypes


def mxq(x, axis, fmt="e4m3"):
    dtype, down = {"e4m3": (ml_dtypes.float8_e4m3fn, 7), "e5m2": (ml_dtypes.float8_e5m2, 14)}[fmt]
    v = np.moveaxis(np.asarray(x, np.float32).astype(ml_dtypes.bfloat16).astype(np.float64), axis, -1)
    blocks = v.reshape(v.shape[:-1] + (-1, 32))
    amax = np.abs(blocks).max(-1, keepdims=True)
    byte = np.maximum(np.where(amax > 0, np.frexp(amax)[1] - 1 + 127, 0) - down, 1)
    scale = np.exp2(byte - 127.0)
    codes = (blocks / scale).astype(np.float32).astype(dtype).astype(np.float64)
    return np.moveaxis((codes * scale).reshape(v.shape), -1, axis)


WIDE = False


def mx_kscale(k):
    if not WIDE:
        return np.ones(k)
    levels = np.array([30, -30])
    if k % 512:
        return np.exp2(np.random.permutation(np.resize(levels, k // 32))).repeat(32)
    a = np.empty((k // 512, 16))
    for p in range(k // 512):
        a[p, :8] = np.random.permutation(np.resize(levels, 8))
        for g in range(8):
            far = levels[np.abs(levels - a[p, g]) >= 10]
            a[p, g + 8] = far[np.random.randint(len(far))]
    return np.exp2(a.ravel()).repeat(32)


BF16 = ml_dtypes.bfloat16


def bf(x):
    return np.asarray(x, np.float32).astype(BF16)


def f64(x):
    return np.asarray(x).astype(np.float64)


E2M1 = np.array([0.0, 0.5, 1.0, 1.5, 2.0, 3.0, 4.0, 6.0, -0.0, -0.5, -1.0, -1.5, -2.0, -3.0, -4.0, -6.0])


def pack_weight(w, fmt):
    k, n = w.shape
    w = f64(bf(w)).reshape(k // 32, 32, n)
    amax = np.abs(w).max(1)
    if fmt in ("e4m3", "e5m2"):
        byte = np.frexp(amax)[1] - 1 + 127 - (7 if fmt == "e4m3" else 14)
    else:
        mant, ex = np.frexp(amax / 6.0)
        byte = np.where(mant > 0.5, ex, ex - 1) + 127
    byte = np.clip(np.where(amax > 0, byte, 1), 1, 254)
    scaled = (w * np.exp2(127.0 - byte)[:, None, :]).reshape(k, n).astype(np.float32)
    by_word = np.ascontiguousarray(scaled.reshape(k // 512, 128, 4, n).transpose(0, 1, 3, 2))
    if fmt in ("e4m3", "e5m2"):
        words = by_word.astype(ml_dtypes.float8_e4m3fn if fmt == "e4m3" else ml_dtypes.float8_e5m2).view(np.uint8)
    else:
        c = by_word.astype(ml_dtypes.float4_e2m1fn).view(np.uint8) & 0xF
        words = c[..., 0::2] | (c[..., 1::2] << 4)
    return np.ascontiguousarray(words), np.ascontiguousarray(byte.astype(np.uint8).reshape(k // 512, 16, n))


def unpack_weight(words, scales, fmt):
    g, p, n, _ = words.shape
    if fmt in ("e4m3", "e5m2"):
        vals = np.ascontiguousarray(words).view(ml_dtypes.float8_e4m3fn if fmt == "e4m3" else ml_dtypes.float8_e5m2).astype(np.float64)
    else:
        nib = np.empty((g, p, n, 4), np.uint8)
        nib[..., 0::2] = words & 0xF
        nib[..., 1::2] = words >> 4
        vals = E2M1[nib]
    vals = vals * np.repeat(np.exp2(scales.astype(np.float64) - 127.0), 8, axis=1)[..., None]
    return vals.transpose(0, 1, 3, 2).reshape(g * 512, n)


T, B, H, K, N = 64, 64, 512, 4096, 1536

MU = 0.9


def setup_inputs():
    s = mx_kscale(K)
    h = np.tanh(np.random.standard_normal((K, H))) * s[:, None]
    G = np.random.standard_t(5, (K, N)) / np.sqrt(K) / s[:, None]
    G_words, G_scales = pack_weight(G, "e5m2")
    return {"h0": bf(h[:B]),
            "h_seq": bf(h[B:].reshape(T - 1, B, H)),
            "g_words": G_words,
            "g_scales": G_scales,
            "rate": bf(1 + 0.1 * np.random.standard_normal(N)),
            "v": bf(np.random.standard_normal((H, N))),
            "u": bf(np.random.standard_normal((H, N)))}


def reference(h0, h_seq, g_words, g_scales, rate, v, u):
    h_prev = np.concatenate([f64(h0)[None], f64(h_seq)], axis=0).reshape(K, H)
    G = unpack_weight(g_words, g_scales, "e5m2")
    du = mxq(h_prev, 0, "e4m3").T @ G
    v_new = MU * f64(v) + du * f64(rate)
    u_new = f64(u) - v_new
    return v_new, u_new

@@ -1,0 +1,231 @@
+from contextlib import ExitStack
+
+import concourse.mybir as mybir
+from concourse.masks import make_identity
+
+B, H, K, N = 64, 512, 4096, 1536
+MU = 0.9
+FLOPS = 2 * K * H * N
+
+F32 = mybir.dt.float32
+BF16 = mybir.dt.bfloat16
+I32 = mybir.dt.int32
+U32 = mybir.dt.uint32
+U8 = mybir.dt.uint8
+E4M3X4 = mybir.dt.float8_e4m3fn_x4
+E5M2X4 = mybir.dt.float8_e5m2_x4
+ALU = mybir.AluOpType
+
+P = 128
+PACK = 4
+K_PASS = P * PACK
+PASSES = K // K_PASS
+N_TILE = 512
+CHUNKS = N // N_TILE
+M_TILES = H // P
+RATE_COLS = N // P
+SCALAR_COLS = 256
+PASS_ORDER = [1, 0, 2, 3, 4, 5, 6, 7]
+
+
+def tile_gru_recurrent_momentum_step_e2_kernel(tc, h0, h_seq, g_words, g_scales, rate, v, u, out_0, out_1):
+    nc = tc.nc
+    h_rows = h_seq.rearrange("s b w -> (s b) w")
+    words_hbm = g_words.rearrange("g p n t -> p g (n t)")
+    scales_hbm = g_scales.rearrange("g (q r) n -> r q g n", r=4)
+    v_hbm = v.rearrange("(m p) n -> p m n", p=P)
+    u_hbm = u.rearrange("(m p) n -> p m n", p=P)
+    v_out_hbm = out_0.rearrange("(m p) n -> p m n", p=P)
+    u_out_hbm = out_1.rearrange("(m p) n -> p m n", p=P)
+
+    def cols(n):
+        return slice(n * N_TILE, (n + 1) * N_TILE)
+
+    with ExitStack() as ctx:
+        keep = ctx.enter_context(tc.tile_pool(name="keep", bufs=1))
+        stage = ctx.enter_context(tc.tile_pool(name="stage", bufs=3))
+        psum = ctx.enter_context(tc.psum_pool(name="psum", bufs=1))
+        ctx.enter_context(tc.manual_schedule())
+
+        g_plane = keep.tile([P, PASSES, N], U8, align_bytes=64)
+        nc.vector.memset(g_plane[:].rearrange("p g n -> p (g n)").bitcast(I32), 0)
+
+        rate_rows = keep.tile([P, RATE_COLS], BF16)
+        nc.scalar.dma_start(out=rate_rows[:], in_=rate.rearrange("(p c) -> p c", c=RATE_COLS))
+        ident = keep.tile([P, P], BF16)
+        make_identity(nc, ident[:])
+
+        h_raw, g_codes, v_in, u_in = {}, {}, {}, {}
+
+        def load_h(g0, g1):
+            t = keep.tile([P, g1 - g0, PACK * H], BF16, name="h_raw_%d" % g0)
+            if g0 == 0:
+                first = B // PACK
+                nc.sync.dma_start(out=t[0:first, 0, :], in_=h0.rearrange("(p j) w -> p (j w)", j=PACK))
+                nc.sync.dma_start(
+                    out=t[first:P, 0, :], in_=h_rows[0 : K_PASS - B, :].rearrange("(p j) w -> p (j w)", j=PACK)
+                )
+            else:
+                nc.sync.dma_start(
+                    out=t[:],
+                    in_=h_rows[g0 * K_PASS - B : g1 * K_PASS - B, :].rearrange("(g p j) w -> p g (j w)", p=P, j=PACK),
+                )
+            for g in range(g0, g1):
+                h_raw[g] = t[:, g - g0, :]
+
+        def load_g(n, g0, g1):
+            t = keep.tile([P, g1 - g0, N_TILE], U32, name="g_codes_%d_%d" % (n, g0), align_bytes=64)
+            src = words_hbm[:, g0:g1, n * N_TILE * PACK : (n + 1) * N_TILE * PACK]
+            nc.sync.dma_start(out=t[:].bitcast(I32), in_=src.bitcast(I32))
+            for g in range(g0, g1):
+                g_codes[n, g] = t[:, g - g0, :]
+
+        def load_scales():
+            for r in range(4):
+                nc.sync.dma_start(out=g_plane[r:P:32, :, :].bitcast(I32), in_=scales_hbm[r].bitcast(I32))
+
+        def load_state(store, hbm, n, label):
+            t = keep.tile([P, M_TILES, N_TILE], BF16, name="%s_%d" % (label, n))
+            nc.sync.dma_start(out=t[:], in_=hbm[:, :, cols(n)])
+            store[n] = t
+
+        load_h(1, 2)
+        load_h(0, 1)
+        load_scales()
+        load_g(0, 0, 2)
+        load_h(2, 4)
+        load_h(4, 6)
+        load_g(0, 2, 4)
+        load_h(6, 7)
+        load_g(0, 4, 6)
+        load_h(7, 8)
+        load_g(0, 6, 8)
+        load_g(1, 0, 2)
+        load_state(v_in, v_hbm, 0, "v_in")
+        load_g(1, 2, 4)
+        load_state(u_in, u_hbm, 0, "u_in")
+        load_g(1, 4, 8)
+        load_state(v_in, v_hbm, 1, "v_in")
+        load_state(u_in, u_hbm, 1, "u_in")
+        load_g(2, 0, 4)
+        load_g(2, 4, 8)
+        load_state(v_in, v_hbm, 2, "v_in")
+        load_state(u_in, u_hbm, 2, "u_in")
+
+        rate_all = keep.tile([P, N], F32)
+        rate_banks = []
+        for b in range(RATE_COLS // 4):
+            spread = psum.tile([P, 4, P], BF16, name="spread_%d" % b, tag="bank_%d" % (M_TILES + b))
+            for c in range(4):
+                col = 4 * b + c
+                nc.tensor.transpose(spread[:, c, :], rate_rows[:, col : col + 1].to_broadcast([P, P]), ident[:])
+            rate_banks.append(spread)
+
+        def spread_rate():
+            for b in range(RATE_COLS // 4):
+                nc.scalar.copy(
+                    out=rate_all[:].rearrange("q (p c) -> q p c", c=RATE_COLS)[:, :, 4 * b : 4 * b + 4],
+                    in_=rate_banks[b][:].rearrange("q c p -> q p c"),
+                )
+
+        h_codes = keep.tile([P, PASSES, H], U32, align_bytes=64)
+        h_plane = keep.tile([P, PASSES, H], U8, align_bytes=64)
+        grouped = {}
+
+        def interleave(g):
+            t = stage.tile([P, H, PACK], BF16, name="grouped", align_bytes=64)
+            dst = t[:].rearrange("p (c i) t -> p c t i", i=4)
+            src = h_raw[g].rearrange("p (t c i) -> p c t i", t=PACK, i=4)
+            cut = SCALAR_COLS // 4
+            nc.scalar.copy(out=dst[:, 0:cut], in_=src[:, 0:cut])
+            nc.vector.tensor_copy(out=dst[:, cut:], in_=src[:, cut:])
+            grouped[g] = t
+
+        def quantize(g):
+            nc.vector.quantize_mx(
+                out=h_codes[:, g, :].bitcast(E4M3X4),
+                scales=h_plane[:, g, :],
+                in_=grouped[g][:].rearrange("p w t -> p (w t)"),
+            )
+
+        acc = {}
+
+        def open_banks(n):
+            for m in range(M_TILES):
+                bank = (n % 2) * M_TILES + m
+                acc[n, m] = psum.tile([P, N_TILE], F32, name="acc_%d_%d" % (n, m), tag="bank_%d" % bank)
+
+        def multiply(n, m, g, order):
+            m_cols = slice(m * P, (m + 1) * P)
+            nc.tensor.matmul_mx(
+                out=acc[n, m][:],
+                lhsT=h_codes[:, g, m_cols].bitcast(E4M3X4),
+                lhsT_scale=h_plane[:, g, m_cols],
+                rhs=g_codes[n, g].bitcast(E5M2X4),
+                rhs_scale=g_plane[:, g, cols(n)],
+                start=(g == order[0]),
+                stop=(g == order[-1]),
+            )
+
+        def sweep(n):
+            order = list(range(PASSES))
+            open_banks(n)
+            for g in order[: PASSES // 2]:
+                for m in range(M_TILES):
+                    multiply(n, m, g, order)
+            for m in range(M_TILES):
+                for g in order[PASSES // 2 :]:
+                    multiply(n, m, g, order)
+
+        open_banks(0)
+        for i in range(PASSES + 1):
+            if i < PASSES:
+                interleave(PASS_ORDER[i])
+            if i == 1:
+                spread_rate()
+            if i >= 1:
+                g = PASS_ORDER[i - 1]
+                quantize(g)
+                for m in range(M_TILES):
+                    multiply(0, m, g, PASS_ORDER)
+
+        v_new, u_new, scaled = {}, {}, {}
+        for n in range(CHUNKS):
+            v_new[n] = keep.tile([P, M_TILES, N_TILE], F32, name="v_new_%d" % n)
+            u_new[n] = keep.tile([P, M_TILES, N_TILE], F32, name="u_new_%d" % n)
+
+        def store(hbm, result, n, m):
+            span = 2 if n == CHUNKS - 1 else M_TILES
+            if (m + 1) % span == 0:
+                rows = slice(m + 1 - span, m + 1)
+                nc.sync.dma_start(out=hbm[:, rows, cols(n)], in_=result[n][:, rows, :])
+
+        def scale_step(s):
+            n, m = divmod(s, M_TILES)
+            t = stage.tile([P, N_TILE], F32, name="scaled")
+            nc.vector.tensor_tensor(out=t[:], in0=acc[n, m][:], in1=rate_all[:, cols(n)], op=ALU.mult)
+            scaled[s] = t
+
+        def momentum_step(s):
+            n, m = divmod(s, M_TILES)
+            nc.vector.scalar_tensor_tensor(
+                out=v_new[n][:, m, :], in0=v_in[n][:, m, :], scalar=MU, in1=scaled[s][:], op0=ALU.mult, op1=ALU.add
+            )
+            store(v_out_hbm, v_new, n, m)
+
+        def update_step(s):
+            n, m = divmod(s, M_TILES)
+            nc.vector.tensor_tensor(out=u_new[n][:, m, :], in0=u_in[n][:, m, :], in1=v_new[n][:, m, :], op=ALU.subtract)
+            store(u_out_hbm, u_new, n, m)
+
+        sweep(1)
+        tiles = CHUNKS * M_TILES
+        for s in range(tiles + 2):
+            if s == M_TILES:
+                sweep(2)
+            if s < tiles:
+                scale_step(s)
+            if 1 <= s <= tiles:
+                momentum_step(s - 1)
+            if s >= 2:
+                update_step(s - 2)

@@ -32,7 +32,6 @@ def tile_gru_recurrent_momentum_step_e2_kernel(tc, h0, h_seq, g_words, g_scales,
     nc = tc.nc
     h_rows = h_seq.rearrange("s b w -> (s b) w")
     words_hbm = g_words.rearrange("g p n t -> p g (n t)")
-    scales_hbm = g_scales.rearrange("g (q r) n -> r q g n", r=4)
     v_hbm = v.rearrange("(m p) n -> p m n", p=P)
     u_hbm = u.rearrange("(m p) n -> p m n", p=P)
     v_out_hbm = out_0.rearrange("(m p) n -> p m n", p=P)
@@ -47,8 +46,12 @@ def tile_gru_recurrent_momentum_step_e2_kernel(tc, h0, h_seq, g_words, g_scales,
         psum = ctx.enter_context(tc.psum_pool(name="psum", bufs=1))
         ctx.enter_context(tc.manual_schedule())
 
-        g_plane = keep.tile([P, PASSES, N], U8, align_bytes=64)
-        nc.vector.memset(g_plane[:].rearrange("p g n -> p (g n)").bitcast(I32), 0)
+        half = PASSES // 2
+        g_planes = []
+        for i in range(2):
+            plane = keep.tile([P, half, N], U8, name="g_plane_%d" % i, align_bytes=64)
+            nc.vector.memset(plane[:].rearrange("p g n -> p (g n)").bitcast(I32), 0)
+            g_planes.append(plane)
 
         rate_rows = keep.tile([P, RATE_COLS], BF16)
         nc.scalar.dma_start(out=rate_rows[:], in_=rate.rearrange("(p c) -> p c", c=RATE_COLS))
@@ -57,65 +60,59 @@ def tile_gru_recurrent_momentum_step_e2_kernel(tc, h0, h_seq, g_words, g_scales,
 
         h_raw, g_codes, v_in, u_in = {}, {}, {}, {}
 
-        def load_h(g0, g1):
-            t = keep.tile([P, g1 - g0, PACK * H], BF16, name="h_raw_%d" % g0)
-            if g0 == 0:
+        def load_h(g):
+            t = keep.tile([P, PACK * H], BF16, name="h_raw_%d" % g)
+            if g == 0:
                 first = B // PACK
-                nc.sync.dma_start(out=t[0:first, 0, :], in_=h0.rearrange("(p j) w -> p (j w)", j=PACK))
+                nc.sync.dma_start(out=t[0:first, :], in_=h0.rearrange("(p j) w -> p (j w)", j=PACK))
                 nc.sync.dma_start(
-                    out=t[first:P, 0, :], in_=h_rows[0 : K_PASS - B, :].rearrange("(p j) w -> p (j w)", j=PACK)
+                    out=t[first:P, :], in_=h_rows[0 : K_PASS - B, :].rearrange("(p j) w -> p (j w)", j=PACK)
                 )
             else:
                 nc.sync.dma_start(
                     out=t[:],
-                    in_=h_rows[g0 * K_PASS - B : g1 * K_PASS - B, :].rearrange("(g p j) w -> p g (j w)", p=P, j=PACK),
+                    in_=h_rows[g * K_PASS - B : (g + 1) * K_PASS - B, :].rearrange("(p j) w -> p (j w)", j=PACK),
                 )
-            for g in range(g0, g1):
-                h_raw[g] = t[:, g - g0, :]
+            h_raw[g] = t
 
-        def load_g(n, g0, g1):
-            t = keep.tile([P, g1 - g0, N_TILE], U32, name="g_codes_%d_%d" % (n, g0), align_bytes=64)
-            src = words_hbm[:, g0:g1, n * N_TILE * PACK : (n + 1) * N_TILE * PACK]
+        def load_g(n0, n1, g0, g1):
+            t = keep.tile([P, g1 - g0, (n1 - n0) * N_TILE], U32, name="g_codes_%d_%d" % (n0, g0), align_bytes=64)
+            src = words_hbm[:, g0:g1, n0 * N_TILE * PACK : n1 * N_TILE * PACK]
             nc.sync.dma_start(out=t[:].bitcast(I32), in_=src.bitcast(I32))
             for g in range(g0, g1):
-                g_codes[n, g] = t[:, g - g0, :]
+                for n in range(n0, n1):
+                    g_codes[n, g] = t[:, g - g0, cols(n - n0)]
 
-        def load_scales():
+        def load_scales(i):
             for r in range(4):
-                nc.sync.dma_start(out=g_plane[r:P:32, :, :].bitcast(I32), in_=scales_hbm[r].bitcast(I32))
+                src = g_scales[i * half : (i + 1) * half, r : r + 13, :].rearrange("g j n -> j g n")
+                nc.sync.dma_start(out=g_planes[i][r : r + 97 : 8, :, :].bitcast(I32), in_=src.bitcast(I32))
 
-        def load_state(store, hbm, n, label):
-            t = keep.tile([P, M_TILES, N_TILE], BF16, name="%s_%d" % (label, n))
-            nc.sync.dma_start(out=t[:], in_=hbm[:, :, cols(n)])
-            store[n] = t
+        def load_state(store, hbm, pair, label):
+            t = keep.tile([P, 2, N], BF16, name="%s_%d" % (label, pair))
+            nc.sync.dma_start(out=t[:], in_=hbm[:, 2 * pair : 2 * pair + 2, :])
+            store[pair] = t
 
-        load_h(1, 2)
-        load_h(0, 1)
-        load_scales()
-        load_g(0, 0, 2)
-        load_h(2, 4)
-        load_h(4, 6)
-        load_g(0, 2, 4)
-        load_h(6, 7)
-        load_g(0, 4, 6)
-        load_h(7, 8)
-        load_g(0, 6, 8)
-        load_g(1, 0, 2)
+        load_h(PASS_ORDER[0])
+        load_h(PASS_ORDER[1])
+        load_scales(0)
+        for i in range(PASSES):
+            if i == half:
+                load_scales(1)
+            if 1 <= i < PASSES - 1:
+                load_h(PASS_ORDER[i + 1])
+            load_g(0, 2, PASS_ORDER[i], PASS_ORDER[i] + 1)
         load_state(v_in, v_hbm, 0, "v_in")
-        load_g(1, 2, 4)
+        load_g(2, 3, 0, half)
         load_state(u_in, u_hbm, 0, "u_in")
-        load_g(1, 4, 8)
         load_state(v_in, v_hbm, 1, "v_in")
+        load_g(2, 3, half, PASSES)
         load_state(u_in, u_hbm, 1, "u_in")
-        load_g(2, 0, 4)
-        load_g(2, 4, 8)
-        load_state(v_in, v_hbm, 2, "v_in")
-        load_state(u_in, u_hbm, 2, "u_in")
 
         rate_all = keep.tile([P, N], F32)
         rate_banks = []
         for b in range(RATE_COLS // 4):
-            spread = psum.tile([P, 4, P], BF16, name="spread_%d" % b, tag="bank_%d" % (M_TILES + b))
+            spread = psum.tile([P, 4, P], BF16, name="spread_%d" % b, tag="bank_%d" % (5 + b))
             for c in range(4):
                 col = 4 * b + c
                 nc.tensor.transpose(spread[:, c, :], rate_rows[:, col : col + 1].to_broadcast([P, P]), ident[:])
@@ -135,7 +132,7 @@ def tile_gru_recurrent_momentum_step_e2_kernel(tc, h0, h_seq, g_words, g_scales,
         def interleave(g):
             t = stage.tile([P, H, PACK], BF16, name="grouped", align_bytes=64)
             dst = t[:].rearrange("p (c i) t -> p c t i", i=4)
-            src = h_raw[g].rearrange("p (t c i) -> p c t i", t=PACK, i=4)
+            src = h_raw[g][:].rearrange("p (t c i) -> p c t i", t=PACK, i=4)
             cut = SCALAR_COLS // 4
             nc.scalar.copy(out=dst[:, 0:cut], in_=src[:, 0:cut])
             nc.vector.tensor_copy(out=dst[:, cut:], in_=src[:, cut:])
@@ -150,82 +147,63 @@ def tile_gru_recurrent_momentum_step_e2_kernel(tc, h0, h_seq, g_words, g_scales,
 
         acc = {}
 
-        def open_banks(n):
-            for m in range(M_TILES):
-                bank = (n % 2) * M_TILES + m
-                acc[n, m] = psum.tile([P, N_TILE], F32, name="acc_%d_%d" % (n, m), tag="bank_%d" % bank)
-
         def multiply(n, m, g, order):
+            if g == order[0]:
+                bank = 2 * m + n if n < 2 else m
+                acc[n, m] = psum.tile([P, N_TILE], F32, name="acc_%d_%d" % (n, m), tag="bank_%d" % bank)
             m_cols = slice(m * P, (m + 1) * P)
             nc.tensor.matmul_mx(
                 out=acc[n, m][:],
                 lhsT=h_codes[:, g, m_cols].bitcast(E4M3X4),
                 lhsT_scale=h_plane[:, g, m_cols],
                 rhs=g_codes[n, g].bitcast(E5M2X4),
-                rhs_scale=g_plane[:, g, cols(n)],
+                rhs_scale=g_planes[g // half][:, g % half, cols(n)],
                 start=(g == order[0]),
                 stop=(g == order[-1]),
             )
 
-        def sweep(n):
-            order = list(range(PASSES))
-            open_banks(n)
-            for g in order[: PASSES // 2]:
-                for m in range(M_TILES):
-                    multiply(n, m, g, order)
-            for m in range(M_TILES):
-                for g in order[PASSES // 2 :]:
-                    multiply(n, m, g, order)
-
-        open_banks(0)
-        for i in range(PASSES + 1):
-            if i < PASSES:
-                interleave(PASS_ORDER[i])
-            if i == 1:
+        for i in range(PASSES):
+            g = PASS_ORDER[i]
+            interleave(g)
+            if i == 0:
                 spread_rate()
-            if i >= 1:
-                g = PASS_ORDER[i - 1]
-                quantize(g)
+            quantize(g)
+            for m in range(M_TILES):
+                for n in range(2):
+                    multiply(n, m, g, PASS_ORDER)
+
+        def second_sweep():
+            order = list(range(PASSES))
+            for g in order[:half]:
                 for m in range(M_TILES):
-                    multiply(0, m, g, PASS_ORDER)
+                    multiply(2, m, g, order)
+            for m in range(M_TILES):
+                for g in order[half:]:
+                    multiply(2, m, g, order)
 
-        v_new, u_new, scaled = {}, {}, {}
-        for n in range(CHUNKS):
-            v_new[n] = keep.tile([P, M_TILES, N_TILE], F32, name="v_new_%d" % n)
-            u_new[n] = keep.tile([P, M_TILES, N_TILE], F32, name="u_new_%d" % n)
+        def finish(pair, n0, n1):
+            width = (n1 - n0) * N_TILE
+            span = slice(n0 * N_TILE, n1 * N_TILE)
+            rows = slice(2 * pair, 2 * pair + 2)
+            scaled = stage.tile([P, 2, width], F32, name="scaled", bufs=2)
+            v_new = keep.tile([P, 2, width], F32, name="v_new_%d_%d" % (pair, n0))
+            u_new = keep.tile([P, 2, width], F32, name="u_new_%d_%d" % (pair, n0))
+            for j in range(2):
+                for n in range(n0, n1):
+                    nc.vector.tensor_tensor(
+                        out=scaled[:, j, cols(n - n0)], in0=acc[n, 2 * pair + j][:], in1=rate_all[:, cols(n)], op=ALU.mult
+                    )
+            for j in range(2):
+                nc.vector.scalar_tensor_tensor(
+                    out=v_new[:, j, :], in0=v_in[pair][:, j, span], scalar=MU, in1=scaled[:, j, :], op0=ALU.mult, op1=ALU.add
+                )
+            nc.sync.dma_start(out=v_out_hbm[:, rows, span], in_=v_new[:])
+            for j in range(2):
+                nc.vector.tensor_tensor(out=u_new[:, j, :], in0=u_in[pair][:, j, span], in1=v_new[:, j, :], op=ALU.subtract)
+            nc.sync.dma_start(out=u_out_hbm[:, rows, span], in_=u_new[:])
 
-        def store(hbm, result, n, m):
-            span = 2 if n == CHUNKS - 1 else M_TILES
-            if (m + 1) % span == 0:
-                rows = slice(m + 1 - span, m + 1)
-                nc.sync.dma_start(out=hbm[:, rows, cols(n)], in_=result[n][:, rows, :])
-
-        def scale_step(s):
-            n, m = divmod(s, M_TILES)
-            t = stage.tile([P, N_TILE], F32, name="scaled")
-            nc.vector.tensor_tensor(out=t[:], in0=acc[n, m][:], in1=rate_all[:, cols(n)], op=ALU.mult)
-            scaled[s] = t
-
-        def momentum_step(s):
-            n, m = divmod(s, M_TILES)
-            nc.vector.scalar_tensor_tensor(
-                out=v_new[n][:, m, :], in0=v_in[n][:, m, :], scalar=MU, in1=scaled[s][:], op0=ALU.mult, op1=ALU.add
-            )
-            store(v_out_hbm, v_new, n, m)
-
-        def update_step(s):
-            n, m = divmod(s, M_TILES)
-            nc.vector.tensor_tensor(out=u_new[n][:, m, :], in0=u_in[n][:, m, :], in1=v_new[n][:, m, :], op=ALU.subtract)
-            store(u_out_hbm, u_new, n, m)
-
-        sweep(1)
-        tiles = CHUNKS * M_TILES
-        for s in range(tiles + 2):
-            if s == M_TILES:
-                sweep(2)
-            if s < tiles:
-                scale_step(s)
-            if 1 <= s <= tiles:
-                momentum_step(s - 1)
-            if s >= 2:
-                update_step(s - 2)
+        finish(0, 0, 2)
+        second_sweep()
+        finish(1, 0, 2)
+        finish(0, 2, 3)
+        finish(1, 2, 3)

from contextlib import ExitStack

import concourse.mybir as mybir
from concourse.masks import make_identity

B, H, K, N = 64, 512, 4096, 1536
MU = 0.9
FLOPS = 2 * K * H * N

F32 = mybir.dt.float32
BF16 = mybir.dt.bfloat16
I32 = mybir.dt.int32
U32 = mybir.dt.uint32
U8 = mybir.dt.uint8
E4M3X4 = mybir.dt.float8_e4m3fn_x4
E5M2X4 = mybir.dt.float8_e5m2_x4
ALU = mybir.AluOpType

P = 128
PACK = 4
K_PASS = P * PACK
PASSES = K // K_PASS
N_TILE = 512
CHUNKS = N // N_TILE
M_TILES = H // P
RATE_COLS = N // P
SCALAR_COLS = 256
PASS_ORDER = [1, 0, 2, 3, 4, 5, 6, 7]


def tile_gru_recurrent_momentum_step_e2_kernel(tc, h0, h_seq, g_words, g_scales, rate, v, u, out_0, out_1):
    nc = tc.nc
    h_rows = h_seq.rearrange("s b w -> (s b) w")
    words_hbm = g_words.rearrange("g p n t -> p g (n t)")
    v_hbm = v.rearrange("(m p) n -> p m n", p=P)
    u_hbm = u.rearrange("(m p) n -> p m n", p=P)
    v_out_hbm = out_0.rearrange("(m p) n -> p m n", p=P)
    u_out_hbm = out_1.rearrange("(m p) n -> p m n", p=P)

    def cols(n):
        return slice(n * N_TILE, (n + 1) * N_TILE)

    with ExitStack() as ctx:
        keep = ctx.enter_context(tc.tile_pool(name="keep", bufs=1))
        stage = ctx.enter_context(tc.tile_pool(name="stage", bufs=3))
        psum = ctx.enter_context(tc.psum_pool(name="psum", bufs=1))
        ctx.enter_context(tc.manual_schedule())

        half = PASSES // 2
        g_planes = []
        for i in range(2):
            plane = keep.tile([P, half, N], U8, name="g_plane_%d" % i, align_bytes=64)
            nc.vector.memset(plane[:].rearrange("p g n -> p (g n)").bitcast(I32), 0)
            g_planes.append(plane)

        rate_rows = keep.tile([P, RATE_COLS], BF16)
        nc.scalar.dma_start(out=rate_rows[:], in_=rate.rearrange("(p c) -> p c", c=RATE_COLS))
        ident = keep.tile([P, P], BF16)
        make_identity(nc, ident[:])

        h_raw, g_codes, v_in, u_in = {}, {}, {}, {}

        def load_h(g):
            t = keep.tile([P, PACK * H], BF16, name="h_raw_%d" % g)
            if g == 0:
                first = B // PACK
                nc.sync.dma_start(out=t[0:first, :], in_=h0.rearrange("(p j) w -> p (j w)", j=PACK))
                nc.sync.dma_start(
                    out=t[first:P, :], in_=h_rows[0 : K_PASS - B, :].rearrange("(p j) w -> p (j w)", j=PACK)
                )
            else:
                nc.sync.dma_start(
                    out=t[:],
                    in_=h_rows[g * K_PASS - B : (g + 1) * K_PASS - B, :].rearrange("(p j) w -> p (j w)", j=PACK),
                )
            h_raw[g] = t

        def load_g(n0, n1, g0, g1):
            t = keep.tile([P, g1 - g0, (n1 - n0) * N_TILE], U32, name="g_codes_%d_%d" % (n0, g0), align_bytes=64)
            src = words_hbm[:, g0:g1, n0 * N_TILE * PACK : n1 * N_TILE * PACK]
            nc.sync.dma_start(out=t[:].bitcast(I32), in_=src.bitcast(I32))
            for g in range(g0, g1):
                for n in range(n0, n1):
                    g_codes[n, g] = t[:, g - g0, cols(n - n0)]

        def load_scales(i):
            for r in range(4):
                src = g_scales[i * half : (i + 1) * half, r : r + 13, :].rearrange("g j n -> j g n")
                nc.sync.dma_start(out=g_planes[i][r : r + 97 : 8, :, :].bitcast(I32), in_=src.bitcast(I32))

        def load_state(store, hbm, pair, label):
            t = keep.tile([P, 2, N], BF16, name="%s_%d" % (label, pair))
            nc.sync.dma_start(out=t[:], in_=hbm[:, 2 * pair : 2 * pair + 2, :])
            store[pair] = t

        load_h(PASS_ORDER[0])
        load_h(PASS_ORDER[1])
        load_scales(0)
        for i in range(PASSES):
            if i == half:
                load_scales(1)
            if 1 <= i < PASSES - 1:
                load_h(PASS_ORDER[i + 1])
            load_g(0, 2, PASS_ORDER[i], PASS_ORDER[i] + 1)
        load_state(v_in, v_hbm, 0, "v_in")
        load_g(2, 3, 0, half)
        load_state(u_in, u_hbm, 0, "u_in")
        load_state(v_in, v_hbm, 1, "v_in")
        load_g(2, 3, half, PASSES)
        load_state(u_in, u_hbm, 1, "u_in")

        rate_all = keep.tile([P, N], F32)
        rate_banks = []
        for b in range(RATE_COLS // 4):
            spread = psum.tile([P, 4, P], BF16, name="spread_%d" % b, tag="bank_%d" % (5 + b))
            for c in range(4):
                col = 4 * b + c
                nc.tensor.transpose(spread[:, c, :], rate_rows[:, col : col + 1].to_broadcast([P, P]), ident[:])
            rate_banks.append(spread)

        def spread_rate():
            for b in range(RATE_COLS // 4):
                nc.scalar.copy(
                    out=rate_all[:].rearrange("q (p c) -> q p c", c=RATE_COLS)[:, :, 4 * b : 4 * b + 4],
                    in_=rate_banks[b][:].rearrange("q c p -> q p c"),
                )

        h_codes = keep.tile([P, PASSES, H], U32, align_bytes=64)
        h_plane = keep.tile([P, PASSES, H], U8, align_bytes=64)
        grouped = {}

        def interleave(g):
            t = stage.tile([P, H, PACK], BF16, name="grouped", align_bytes=64)
            dst = t[:].rearrange("p (c i) t -> p c t i", i=4)
            src = h_raw[g][:].rearrange("p (t c i) -> p c t i", t=PACK, i=4)
            cut = SCALAR_COLS // 4
            nc.scalar.copy(out=dst[:, 0:cut], in_=src[:, 0:cut])
            nc.vector.tensor_copy(out=dst[:, cut:], in_=src[:, cut:])
            grouped[g] = t

        def quantize(g):
            nc.vector.quantize_mx(
                out=h_codes[:, g, :].bitcast(E4M3X4),
                scales=h_plane[:, g, :],
                in_=grouped[g][:].rearrange("p w t -> p (w t)"),
            )

        acc = {}

        def multiply(n, m, g, order):
            if g == order[0]:
                bank = 2 * m + n if n < 2 else m
                acc[n, m] = psum.tile([P, N_TILE], F32, name="acc_%d_%d" % (n, m), tag="bank_%d" % bank)
            m_cols = slice(m * P, (m + 1) * P)
            nc.tensor.matmul_mx(
                out=acc[n, m][:],
                lhsT=h_codes[:, g, m_cols].bitcast(E4M3X4),
                lhsT_scale=h_plane[:, g, m_cols],
                rhs=g_codes[n, g].bitcast(E5M2X4),
                rhs_scale=g_planes[g // half][:, g % half, cols(n)],
                start=(g == order[0]),
                stop=(g == order[-1]),
            )

        for i in range(PASSES):
            g = PASS_ORDER[i]
            interleave(g)
            if i == 0:
                spread_rate()
            quantize(g)
            for m in range(M_TILES):
                for n in range(2):
                    multiply(n, m, g, PASS_ORDER)

        def second_sweep():
            order = list(range(PASSES))
            for g in order[:half]:
                for m in range(M_TILES):
                    multiply(2, m, g, order)
            for m in range(M_TILES):
                for g in order[half:]:
                    multiply(2, m, g, order)

        def finish(pair, n0, n1):
            width = (n1 - n0) * N_TILE
            span = slice(n0 * N_TILE, n1 * N_TILE)
            rows = slice(2 * pair, 2 * pair + 2)
            scaled = stage.tile([P, 2, width], F32, name="scaled", bufs=2)
            v_new = keep.tile([P, 2, width], F32, name="v_new_%d_%d" % (pair, n0))
            u_new = keep.tile([P, 2, width], F32, name="u_new_%d_%d" % (pair, n0))
            for j in range(2):
                for n in range(n0, n1):
                    nc.vector.tensor_tensor(
                        out=scaled[:, j, cols(n - n0)], in0=acc[n, 2 * pair + j][:], in1=rate_all[:, cols(n)], op=ALU.mult
                    )
            for j in range(2):
                nc.vector.scalar_tensor_tensor(
                    out=v_new[:, j, :], in0=v_in[pair][:, j, span], scalar=MU, in1=scaled[:, j, :], op0=ALU.mult, op1=ALU.add
                )
            nc.sync.dma_start(out=v_out_hbm[:, rows, span], in_=v_new[:])
            for j in range(2):
                nc.vector.tensor_tensor(out=u_new[:, j, :], in0=u_in[pair][:, j, span], in1=v_new[:, j, :], op=ALU.subtract)
            nc.sync.dma_start(out=u_out_hbm[:, rows, span], in_=u_new[:])

        finish(0, 0, 2)
        second_sweep()
        finish(1, 0, 2)
        finish(0, 2, 3)
        finish(1, 2, 3)
